import numpy as np
import ml_dtypes


def mxq(x, axis, fmt="e4m3"):
    dtype, down = {"e4m3": (ml_dtypes.float8_e4m3fn, 7), "e5m2": (ml_dtypes.float8_e5m2, 14)}[fmt]
    v = np.moveaxis(np.asarray(x, np.float32).astype(ml_dtypes.bfloat16).astype(np.float64), axis, -1)
    blocks = v.reshape(v.shape[:-1] + (-1, 32))
    amax = np.abs(blocks).max(-1, keepdims=True)
    byte = np.maximum(np.where(amax > 0, np.frexp(amax)[1] - 1 + 127, 0) - down, 1)
    scale = np.exp2(byte - 127.0)
    codes = (blocks / scale).astype(np.float32).astype(dtype).astype(np.float64)
    return np.moveaxis((codes * scale).reshape(v.shape), -1, axis)


WIDE = False


def mx_kscale(k):
    if not WIDE:
        return np.ones(k)
    levels = np.array([10, -10, 5, -5, 0])
    if k % 512:
        return np.exp2(np.random.permutation(np.resize(levels, k // 32))).repeat(32)
    a = np.empty((k // 512, 16))
    for p in range(k // 512):
        a[p, :8] = np.random.permutation(np.resize(levels, 8))
        for g in range(8):
            far = levels[np.abs(levels - a[p, g]) >= 10]
            a[p, g + 8] = far[np.random.randint(len(far))]
    return np.exp2(a.ravel()).repeat(32)


def f64(x):
    return np.asarray(x).astype(np.float64)


def striped(idx):
    return np.tile(idx.reshape(-1, 16).T, (8, 1)).astype(np.uint16)


def unstriped(offs):
    return offs[:16].T.reshape(-1).astype(np.int64)


def pack_weight(w):
    k, n = w.shape
    w = f64(np.asarray(w, np.float32).astype(ml_dtypes.bfloat16)).reshape(k // 32, 32, n)
    amax = np.abs(w).max(1)
    byte = np.clip(np.where(amax > 0, np.frexp(amax)[1] - 1 + 127 - 7, 1), 1, 254)
    scaled = (w * np.exp2(127.0 - byte)[:, None, :]).reshape(k, n).astype(np.float32)
    words = np.ascontiguousarray(scaled.reshape(k // 512, 128, 4, n).transpose(0, 1, 3, 2)).astype(ml_dtypes.float8_e4m3fn).view(np.uint8)
    return words, np.ascontiguousarray(byte.astype(np.uint8).reshape(k // 512, 16, n))


def unpack_weight(words, scales):
    g, p, n, _ = words.shape
    vals = np.ascontiguousarray(words).view(ml_dtypes.float8_e4m3fn).astype(np.float64) * np.repeat(np.exp2(scales.astype(np.float64) - 127.0), 8, axis=1)[..., None]
    return vals.transpose(0, 1, 3, 2).reshape(g * 512, n)


K, T, S, N, H, U = 512, 2048, 512, 128, 512, 1024


def setup_inputs():
    n = np.random.standard_normal
    s = mx_kscale(K)[:, None]
    u = mx_kscale(H)
    packed_xT = pack_weight(n((K, T)) * s)
    return {
        "x_words": packed_xT[0],
        "x_scales": packed_xT[1],
        "w1": (n((K, H)) / np.sqrt(K) / s).astype(np.float32),
        "w2": (n((K, H)) / np.sqrt(K) / s).astype(np.float32),
        "unit": (np.random.uniform(0.6, 1.4, (H, 1)) * u[:, None]).astype(np.float32),
        "w3": (n((H, N)) / np.sqrt(H) / u[:, None]).astype(np.float32),
        "offs": striped(np.random.permutation(T)[:S]),
        "u1": striped(np.random.permutation(np.concatenate([np.arange(S), np.random.randint(0, S, U - S)]))),
        "u2": striped(np.random.permutation(np.concatenate([np.arange(S), np.random.randint(0, S, U - S)]))),
    }


def reference(x_words, x_scales, w1, w2, unit, w3, offs, u1, u2):
    xq = unpack_weight(x_words, x_scales)[:, unstriped(offs)]
    y = mxq(f64(w1), 0, "e4m3").T @ xq
    y1 = y[:, unstriped(u1)]
    z1 = mxq(f64(w2), 0, "e4m3").T @ xq
    z2 = z1[:, unstriped(u2)]
    rep1 = y1 - (0.6 * z2)
    zu = z1[:, unstriped(u1)]
    ctxh = rep1 * zu
    y2 = y[:, unstriped(u2)]
    hid = f64(unit) * (ctxh + y2)
    return mxq(f64(w3), 0, "e4m3").T @ mxq(hid, 0, "e4m3")

@@ -1,0 +1,194 @@
+from contextlib import ExitStack
+
+import concourse.mybir as mybir
+
+F32 = mybir.dt.float32
+BF16 = mybir.dt.bfloat16
+I32 = mybir.dt.int32
+U32 = mybir.dt.uint32
+U16 = mybir.dt.uint16
+U8 = mybir.dt.uint8
+FP8X4 = mybir.dt.float8_e4m3fn_x4
+COPY = mybir.ActivationFunctionType.Copy
+ADD = mybir.AluOpType.add
+MULT = mybir.AluOpType.mult
+
+P = 128
+T, S, H, N, U = 2048, 512, 512, 128, 1024
+FLOPS = 2 * (2 * 512 * H * S + H * N * U)
+CHUNKS = [(0, 384), (384, 384), (768, 256)]
+
+
+def tile_picked_ybackpt_ctx_p_kernel(
+    tc, x_words, x_scales, w1, w2, unit, w3, offs, u1, u2, out
+):
+    nc = tc.nc
+    with ExitStack() as ctx:
+        keep = ctx.enter_context(tc.tile_pool(name="keep", bufs=1))
+        acc_pool = ctx.enter_context(tc.psum_pool(name="acc", bufs=1))
+        out_pool = ctx.enter_context(tc.psum_pool(name="res", bufs=4))
+
+        offs_sb = keep.tile([P, S // 16], U16, name="offs_sb")
+        u1_sb = keep.tile([P, U // 16], U16, name="u1_sb")
+        u2_sb = keep.tile([P, U // 16], U16, name="u2_sb")
+        unit_sb = keep.tile([P, 4], F32, name="unit_sb")
+        x_word_table = keep.tile([P, T], I32, name="x_word_table")
+        x_scale_table = keep.tile([P, T], U8, name="x_scale_table")
+        w1_raw = keep.tile([P, 4, H], F32, name="w1_raw")
+        w2_raw = keep.tile([P, 4, H], F32, name="w2_raw")
+        w3_raw = keep.tile([P, 4, N], F32, name="w3_raw")
+
+        nc.vector.memset(x_scale_table[:].bitcast(I32), 0)
+        nc.sync.dma_start(out=unit_sb[:], in_=unit.rearrange("(p t) one -> p (t one)", t=4))
+        nc.sync.dma_start(out=w1_raw[:], in_=w1.rearrange("(p j) c -> p j c", j=4))
+        for q in range(4):
+            nc.sync.dma_start(
+                out=x_scale_table[32 * q : 32 * q + 4, :].bitcast(I32),
+                in_=x_scales[0, 4 * q : 4 * q + 4, :].bitcast(I32),
+            )
+        nc.sync.dma_start(offs_sb[:], offs)
+        nc.sync.dma_start(out=x_word_table[:], in_=x_words[0].rearrange("p n t -> p (n t)").bitcast(I32))
+        nc.sync.dma_start(u1_sb[:], u1)
+        nc.sync.dma_start(out=w2_raw[:], in_=w2.rearrange("(p j) c -> p j c", j=4))
+        nc.sync.dma_start(u2_sb[:], u2)
+        nc.sync.dma_start(out=w3_raw[:], in_=w3.rearrange("(p j) c -> p j c", j=4))
+
+        cross_gain = keep.tile([P, 4], F32, name="cross_gain")
+        nc.scalar.activation(cross_gain[:], unit_sb[:], COPY, scale=-0.6)
+
+        def round_pair(copy, raw, pair, name):
+            grouped = keep.tile([P, 2, P, 4], BF16, name=name, align_bytes=64)
+            copy(
+                out=grouped[:].rearrange("p e m j -> p m j e"),
+                in_=raw[:].rearrange("p j (m u e) -> p u m j e", u=2, e=2)[:, pair],
+            )
+            return grouped[:].rearrange("p e m j -> p (e m j)")
+
+        def quantise(grouped, width, name):
+            codes = keep.tile([P, width], U32, name=name + "_codes", align_bytes=64)
+            scales = keep.tile([P, width], U8, name=name + "_scales", align_bytes=64)
+            nc.vector.quantize_mx(out=codes[:].bitcast(FP8X4), scales=scales[:], in_=grouped)
+            return codes, scales
+
+        def product(dst, lhs, lhs_cols, rhs, rhs_cols):
+            nc.tensor.matmul_mx(
+                out=dst,
+                lhsT=lhs[0][:, lhs_cols].bitcast(FP8X4),
+                lhsT_scale=lhs[1][:, lhs_cols],
+                rhs=rhs[0][:, rhs_cols].bitcast(FP8X4),
+                rhs_scale=rhs[1][:, rhs_cols],
+                start=True,
+                stop=True,
+            )
+
+        w1_lo = round_pair(nc.vector.tensor_copy, w1_raw, 0, "w1_lo")
+        w1_hi = round_pair(nc.scalar.copy, w1_raw, 1, "w1_hi")
+        w1_q = [quantise(w1_lo, 2 * P, "w1_lo"), quantise(w1_hi, 2 * P, "w1_hi")]
+
+        x_codes = keep.tile([P, S], U32, name="x_codes", align_bytes=64)
+        x_bytes = keep.tile([P, S], U8, name="x_bytes", align_bytes=64)
+        nc.vector.tensor_copy(x_bytes[:], x_scale_table[:].indirect(offs_sb[:]))
+        nc.vector.tensor_copy(x_codes[:], x_word_table[:].bitcast(U32).indirect(offs_sb[:]))
+        x_q = (x_codes, x_bytes)
+
+        def project(w_q, t, bank):
+            acc = acc_pool.tile([P, S], F32, name="acc%d" % bank)
+            product(acc[:], w_q[t // 2], slice((t % 2) * P, (t % 2 + 1) * P), x_q, slice(0, S))
+            return acc
+
+        def window(name):
+            return keep.tile([P, S], F32, name=name)
+
+        def picks(list_sb, k):
+            first, n = CHUNKS[k]
+            return list_sb[:, first // 16 : (first + n) // 16]
+
+        own = [keep.tile([P, 4, n], F32, name="own%d" % k) for k, (first, n) in enumerate(CHUNKS)]
+        other = own
+        rep = [keep.tile([P, 4, n], F32, name="rep%d" % k) for k, (first, n) in enumerate(CHUNKS)]
+        ctxh = [keep.tile([P, 4, n], F32, name="ctxh%d" % k) for k, (first, n) in enumerate(CHUNKS)]
+        y_win = [window("y_win%d" % t) for t in range(4)]
+        z_win = [window("z_win%d" % t) for t in range(4)]
+        c_win = [window("c_win%d" % t) for t in range(4)]
+
+        def y_stage(t, y_acc):
+            nc.scalar.activation(y_win[t][:], y_acc[:], COPY, scale=unit_sb[:, t : t + 1])
+
+        def own_gather(t, k):
+            nc.scalar.activation(own[k][:, t, :], y_win[t][:].indirect(picks(u1_sb, k)), COPY)
+
+        def other_gather(t, k):
+            nc.scalar.activation(other[k][:, t, :], y_win[t][:].indirect(picks(u2_sb, k)), COPY)
+
+        def rep_gather(t, k):
+            nc.vector.tensor_tensor(rep[k][:, t, :], c_win[t][:].indirect(picks(u2_sb, k)), own[k][:, t, :], ADD)
+
+        def ctx_gather(t, k):
+            nc.vector.tensor_tensor(ctxh[k][:, t, :], z_win[t][:].indirect(picks(u1_sb, k)), rep[k][:, t, :], MULT)
+
+        def hid_round(k, a, n):
+            hid = keep.tile([P, n, 4], BF16, name="hid%d_%d" % (k, a), align_bytes=64)
+            nc.vector.tensor_tensor(
+                hid[:].rearrange("p (c i) t -> p c t i", i=2),
+                ctxh[k][:, :, a : a + n].rearrange("p t (c i) -> p c t i", i=2),
+                other[k][:, :, a : a + n].rearrange("p t (c i) -> p c t i", i=2),
+                ADD,
+            )
+            return hid[:].rearrange("p r t -> p (r t)")
+
+        def finish(first, n, hid, w3_q):
+            hid_q = quantise(hid, n, "hid%d" % first)
+            res = out_pool.tile([P, n], F32, name="res")
+            for a in range(0, n, 256):
+                cols = slice(a, min(a + 256, n))
+                product(res[:, cols], w3_q, slice(0, N), hid_q, cols)
+            res_sb = keep.tile([P, n], F32, name="res_sb%d" % first)
+            nc.scalar.copy(out=res_sb[:], in_=res[:])
+            nc.sync.dma_start(out=out[:, first : first + n], in_=res_sb[:])
+
+        y_stage(0, project(w1_q, 0, 0))
+        for k in range(3):
+            own_gather(0, k)
+
+        w2_q = [quantise(round_pair(nc.vector.tensor_copy, w2_raw, 0, "w2_pair"), 2 * P, "w2_lo")]
+        z_acc = [project(w2_q, 0, 1), project(w2_q, 1, 2)]
+        w2_q.append(quantise(round_pair(nc.vector.tensor_copy, w2_raw, 1, "w2_pair"), 2 * P, "w2_hi"))
+        z_acc.extend([project(w2_q, 2, 3), project(w2_q, 3, 0)])
+        nc.vector.tensor_scalar(c_win[0][:], z_acc[0][:], cross_gain[:, 0:1], None, MULT)
+        nc.scalar.copy(out=z_win[0][:], in_=z_acc[0][:])
+
+        for t in range(4):
+            if t > 0:
+                y_stage(t, project(w1_q, t, t))
+                nc.scalar.activation(c_win[t][:], z_acc[t][:], COPY, scale=cross_gain[:, t : t + 1])
+                own_gather(t, 0)
+                nc.scalar.copy(out=z_win[t][:], in_=z_acc[t][:])
+                own_gather(t, 1)
+                own_gather(t, 2)
+            for k in range(3):
+                rep_gather(t, k)
+            if t < 3:
+                for k in range(3):
+                    ctx_gather(t, k)
+
+        w3_grouped = keep.tile([P, N, 4], BF16, name="w3_grouped", align_bytes=64)
+        nc.scalar.copy(
+            out=w3_grouped[:].rearrange("p (c i) j -> p c j i", i=2),
+            in_=w3_raw[:].rearrange("p j (c i) -> p c j i", i=2),
+        )
+        w3_q = quantise(w3_grouped[:].rearrange("p m j -> p (m j)"), N, "w3")
+
+        for k in range(3):
+            for t in range(4):
+                other_gather(t, k)
+        ctx_gather(3, 0)
+        ctx_gather(3, 1)
+        hid0 = hid_round(0, 0, 384)
+        ctx_gather(3, 2)
+        finish(0, 384, hid0, w3_q)
+        hid1 = hid_round(1, 0, 384)
+        hid2 = hid_round(2, 0, 128)
+        finish(384, 384, hid1, w3_q)
+        hid3 = hid_round(2, 128, 128)
+        finish(768, 128, hid2, w3_q)
+        finish(896, 128, hid3, w3_q)

@@ -16,7 +16,9 @@ MULT = mybir.AluOpType.mult
 P = 128
 T, S, H, N, U = 2048, 512, 512, 128, 1024
 FLOPS = 2 * (2 * 512 * H * S + H * N * U)
-CHUNKS = [(0, 384), (384, 384), (768, 256)]
+PAD = 16
+HALVES = [(0, 512), (512, 512)]
+CHUNKS = [(0, 384), (384, 384), (768, 128), (896, 128)]
 
 
 def tile_picked_ybackpt_ctx_p_kernel(
@@ -26,7 +28,7 @@ def tile_picked_ybackpt_ctx_p_kernel(
     with ExitStack() as ctx:
         keep = ctx.enter_context(tc.tile_pool(name="keep", bufs=1))
         acc_pool = ctx.enter_context(tc.psum_pool(name="acc", bufs=1))
-        out_pool = ctx.enter_context(tc.psum_pool(name="res", bufs=4))
+        out_pool = ctx.enter_context(tc.psum_pool(name="res", bufs=3))
 
         offs_sb = keep.tile([P, S // 16], U16, name="offs_sb")
         u1_sb = keep.tile([P, U // 16], U16, name="u1_sb")
@@ -39,12 +41,12 @@ def tile_picked_ybackpt_ctx_p_kernel(
         w3_raw = keep.tile([P, 4, N], F32, name="w3_raw")
 
         nc.vector.memset(x_scale_table[:].bitcast(I32), 0)
-        nc.sync.dma_start(out=unit_sb[:], in_=unit.rearrange("(p t) one -> p (t one)", t=4))
+        nc.scalar.dma_start(out=unit_sb[:], in_=unit.rearrange("(p t) one -> p (t one)", t=4))
         nc.sync.dma_start(out=w1_raw[:], in_=w1.rearrange("(p j) c -> p j c", j=4))
-        for q in range(4):
+        for r in range(4):
             nc.sync.dma_start(
-                out=x_scale_table[32 * q : 32 * q + 4, :].bitcast(I32),
-                in_=x_scales[0, 4 * q : 4 * q + 4, :].bitcast(I32),
+                out=x_scale_table[r:P:32, :].bitcast(I32),
+                in_=x_scales[0].rearrange("(q r) c -> r q c", r=4)[r].bitcast(I32),
             )
         nc.sync.dma_start(offs_sb[:], offs)
         nc.sync.dma_start(out=x_word_table[:], in_=x_words[0].rearrange("p n t -> p (n t)").bitcast(I32))
@@ -56,12 +58,16 @@ def tile_picked_ybackpt_ctx_p_kernel(
         cross_gain = keep.tile([P, 4], F32, name="cross_gain")
         nc.scalar.activation(cross_gain[:], unit_sb[:], COPY, scale=-0.6)
 
-        def round_pair(copy, raw, pair, name):
-            grouped = keep.tile([P, 2, P, 4], BF16, name=name, align_bytes=64)
+        def pair_tile(name):
+            return keep.tile([P, 2, P, 4], BF16, name=name, align_bytes=64)
+
+        def round_pair(copy, grouped, rows, raw, pair):
             copy(
-                out=grouped[:].rearrange("p e m j -> p m j e"),
+                out=grouped[:, :, rows, :].rearrange("p e m j -> p m j e"),
                 in_=raw[:].rearrange("p j (m u e) -> p u m j e", u=2, e=2)[:, pair],
             )
+
+        def flat(grouped):
             return grouped[:].rearrange("p e m j -> p (e m j)")
 
         def quantise(grouped, width, name):
@@ -81,14 +87,19 @@ def tile_picked_ybackpt_ctx_p_kernel(
                 stop=True,
             )
 
-        w1_lo = round_pair(nc.vector.tensor_copy, w1_raw, 0, "w1_lo")
-        w1_hi = round_pair(nc.scalar.copy, w1_raw, 1, "w1_hi")
-        w1_q = [quantise(w1_lo, 2 * P, "w1_lo"), quantise(w1_hi, 2 * P, "w1_hi")]
+        w1_pairs = [pair_tile("w1_lo"), pair_tile("w1_hi")]
+        round_pair(nc.vector.tensor_copy, w1_pairs[0], slice(0, P), w1_raw, 0)
+        round_pair(nc.scalar.copy, w1_pairs[1], slice(0, P), w1_raw, 1)
+        w1_q = [quantise(flat(w1_pairs[0]), 2 * P, "w1_lo"), quantise(flat(w1_pairs[1]), 2 * P, "w1_hi")]
 
-        x_codes = keep.tile([P, S], U32, name="x_codes", align_bytes=64)
         x_bytes = keep.tile([P, S], U8, name="x_bytes", align_bytes=64)
         nc.vector.tensor_copy(x_bytes[:], x_scale_table[:].indirect(offs_sb[:]))
-        nc.vector.tensor_copy(x_codes[:], x_word_table[:].bitcast(U32).indirect(offs_sb[:]))
+        x_codes = keep.tile([P, S], U32, name="x_codes", align_bytes=64)
+        for h in range(2):
+            nc.vector.tensor_copy(
+                x_codes[:, h * 256 : (h + 1) * 256],
+                x_word_table[:].bitcast(U32).indirect(offs_sb[:, h * 16 : (h + 1) * 16]),
+            )
         x_q = (x_codes, x_bytes)
 
         def project(w_q, t, bank):
@@ -97,98 +108,122 @@ def tile_picked_ybackpt_ctx_p_kernel(
             return acc
 
         def window(name):
-            return keep.tile([P, S], F32, name=name)
+            win = keep.tile([P, S + PAD], F32, name=name, align_bytes=64)
+            nc.vector.memset(win[:, S:], 0.0)
+            return win
 
-        def picks(list_sb, k):
-            first, n = CHUNKS[k]
+        def picks(list_sb, part):
+            first, n = part
             return list_sb[:, first // 16 : (first + n) // 16]
 
-        own = [keep.tile([P, 4, n], F32, name="own%d" % k) for k, (first, n) in enumerate(CHUNKS)]
-        other = own
-        rep = [keep.tile([P, 4, n], F32, name="rep%d" % k) for k, (first, n) in enumerate(CHUNKS)]
-        ctxh = [keep.tile([P, 4, n], F32, name="ctxh%d" % k) for k, (first, n) in enumerate(CHUNKS)]
+        def cols(tile, t, part):
+            first, n = part
+            return tile[:, t, first : first + n]
+
+        picked_y = keep.tile([P, 4, U], F32, name="picked_y")
+        rep = keep.tile([P, 4, U], F32, name="rep")
+        ctxh = keep.tile([P, 4, U], F32, name="ctxh")
         y_win = [window("y_win%d" % t) for t in range(4)]
         z_win = [window("z_win%d" % t) for t in range(4)]
         c_win = [window("c_win%d" % t) for t in range(4)]
 
         def y_stage(t, y_acc):
-            nc.scalar.activation(y_win[t][:], y_acc[:], COPY, scale=unit_sb[:, t : t + 1])
+            nc.scalar.activation(y_win[t][:, 0:S], y_acc[:], COPY, scale=unit_sb[:, t : t + 1])
 
-        def own_gather(t, k):
-            nc.scalar.activation(own[k][:, t, :], y_win[t][:].indirect(picks(u1_sb, k)), COPY)
+        def y_gather(t, list_sb, part):
+            nc.scalar.activation(cols(picked_y, t, part), y_win[t][:].indirect(picks(list_sb, part)), COPY)
 
-        def other_gather(t, k):
-            nc.scalar.activation(other[k][:, t, :], y_win[t][:].indirect(picks(u2_sb, k)), COPY)
-
-        def rep_gather(t, k):
-            nc.vector.tensor_tensor(rep[k][:, t, :], c_win[t][:].indirect(picks(u2_sb, k)), own[k][:, t, :], ADD)
-
-        def ctx_gather(t, k):
-            nc.vector.tensor_tensor(ctxh[k][:, t, :], z_win[t][:].indirect(picks(u1_sb, k)), rep[k][:, t, :], MULT)
-
-        def hid_round(k, a, n):
-            hid = keep.tile([P, n, 4], BF16, name="hid%d_%d" % (k, a), align_bytes=64)
+        def rep_gather(t, part):
             nc.vector.tensor_tensor(
-                hid[:].rearrange("p (c i) t -> p c t i", i=2),
-                ctxh[k][:, :, a : a + n].rearrange("p t (c i) -> p c t i", i=2),
-                other[k][:, :, a : a + n].rearrange("p t (c i) -> p c t i", i=2),
+                cols(rep, t, part), c_win[t][:].indirect(picks(u2_sb, part)), cols(picked_y, t, part), ADD
+            )
+
+        def ctx_gather(t, part):
+            nc.vector.tensor_tensor(
+                cols(ctxh, t, part), z_win[t][:].indirect(picks(u1_sb, part)), cols(rep, t, part), MULT
+            )
+
+        def hid_round(part):
+            first, n = part
+            hid = keep.tile([P, n, 4], BF16, name="hid%d" % first, align_bytes=64)
+            nc.vector.tensor_tensor(
+                hid[:].rearrange("p (c i) t -> p c t i", i=4),
+                ctxh[:, :, first : first + n].rearrange("p t (c i) -> p c t i", i=4),
+                picked_y[:, :, first : first + n].rearrange("p t (c i) -> p c t i", i=4),
                 ADD,
             )
             return hid[:].rearrange("p r t -> p (r t)")
 
-        def finish(first, n, hid, w3_q):
+        def finish(part, hid, w3_q):
+            first, n = part
             hid_q = quantise(hid, n, "hid%d" % first)
             res = out_pool.tile([P, n], F32, name="res")
             for a in range(0, n, 256):
-                cols = slice(a, min(a + 256, n))
-                product(res[:, cols], w3_q, slice(0, N), hid_q, cols)
+                piece = slice(a, min(a + 256, n))
+                product(res[:, piece], w3_q, slice(0, N), hid_q, piece)
             res_sb = keep.tile([P, n], F32, name="res_sb%d" % first)
             nc.scalar.copy(out=res_sb[:], in_=res[:])
-            nc.sync.dma_start(out=out[:, first : first + n], in_=res_sb[:])
+            queue = nc.scalar if first + n == U else nc.sync
+            queue.dma_start(out=out[:, first : first + n], in_=res_sb[:])
 
-        y_stage(0, project(w1_q, 0, 0))
-        for k in range(3):
-            own_gather(0, k)
+        for h in range(2):
+            half = slice(h * 256, (h + 1) * 256)
+            acc = acc_pool.tile([P, 256], F32, name="acc%d" % (3 * h))
+            product(acc[:], w1_q[0], slice(0, P), x_q, half)
+            nc.scalar.activation(y_win[0][:, half], acc[:], COPY, scale=unit_sb[:, 0:1])
+        for part in HALVES:
+            y_gather(0, u1_sb, part)
 
-        w2_q = [quantise(round_pair(nc.vector.tensor_copy, w2_raw, 0, "w2_pair"), 2 * P, "w2_lo")]
-        z_acc = [project(w2_q, 0, 1), project(w2_q, 1, 2)]
-        w2_q.append(quantise(round_pair(nc.vector.tensor_copy, w2_raw, 1, "w2_pair"), 2 * P, "w2_hi"))
-        z_acc.extend([project(w2_q, 2, 3), project(w2_q, 3, 0)])
-        nc.vector.tensor_scalar(c_win[0][:], z_acc[0][:], cross_gain[:, 0:1], None, MULT)
-        nc.scalar.copy(out=z_win[0][:], in_=z_acc[0][:])
+        w2_pair = pair_tile("w2_pair")
+        round_pair(nc.vector.tensor_copy, w2_pair, slice(0, P), w2_raw, 0)
+        w2_first = quantise(flat(w2_pair)[:, 0 : 4 * P], P, "w2_first")
+        w2_second = quantise(flat(w2_pair)[:, 4 * P : 8 * P], P, "w2_second")
+        w2_pair = pair_tile("w2_pair")
+        round_pair(nc.vector.tensor_copy, w2_pair, slice(0, P), w2_raw, 1)
+        z_halves = []
+        for h in range(2):
+            half = slice(h * 256, (h + 1) * 256)
+            acc = acc_pool.tile([P, 256], F32, name="acc%d" % (1 + 3 * h))
+            product(acc[:], w2_first, slice(0, P), x_q, half)
+            nc.vector.tensor_scalar(c_win[0][:, half], acc[:], cross_gain[:, 0:1], None, MULT)
+            z_halves.append(acc)
+        for h in range(2):
+            nc.scalar.copy(out=z_win[0][:, h * 256 : (h + 1) * 256], in_=z_halves[h][:])
+        w2_hi = quantise(flat(w2_pair), 2 * P, "w2_hi")
+        w2_q = [None, (w2_second, 0), (w2_hi, 0), (w2_hi, P)]
+        z_acc = [None]
+        for t in range(1, 4):
+            acc = acc_pool.tile([P, S], F32, name="acc%d" % ((t + 1) % 4))
+            product(acc[:], w2_q[t][0], slice(w2_q[t][1], w2_q[t][1] + P), x_q, slice(0, S))
+            z_acc.append(acc)
 
         for t in range(4):
             if t > 0:
+                nc.scalar.copy(out=z_win[t][:, 0:S], in_=z_acc[t][:])
                 y_stage(t, project(w1_q, t, t))
-                nc.scalar.activation(c_win[t][:], z_acc[t][:], COPY, scale=cross_gain[:, t : t + 1])
-                own_gather(t, 0)
-                nc.scalar.copy(out=z_win[t][:], in_=z_acc[t][:])
-                own_gather(t, 1)
-                own_gather(t, 2)
-            for k in range(3):
-                rep_gather(t, k)
-            if t < 3:
-                for k in range(3):
-                    ctx_gather(t, k)
+                if t == 1:
+                    nc.vector.tensor_scalar(c_win[t][:, 0:S], z_win[t][:, 0:S], cross_gain[:, t : t + 1], None, MULT)
+                else:
+                    nc.scalar.activation(c_win[t][:, 0:S], z_acc[t][:], COPY, scale=cross_gain[:, t : t + 1])
+                for part in HALVES:
+                    y_gather(t, u1_sb, part)
+            for part in HALVES:
+                rep_gather(t, part)
+            for part in HALVES:
+                ctx_gather(t, part)
 
-        w3_grouped = keep.tile([P, N, 4], BF16, name="w3_grouped", align_bytes=64)
+        w3_grouped = keep.tile([P, N, 4], BF16, name="w3_grouped", tag="z_win1", align_bytes=64)
         nc.scalar.copy(
-            out=w3_grouped[:].rearrange("p (c i) j -> p c j i", i=2),
-            in_=w3_raw[:].rearrange("p j (c i) -> p c j i", i=2),
+            out=w3_grouped[:].rearrange("p (c i) j -> p c j i", i=4),
+            in_=w3_raw[:].rearrange("p j (c i) -> p c j i", i=4),
         )
         w3_q = quantise(w3_grouped[:].rearrange("p m j -> p (m j)"), N, "w3")
 
-        for k in range(3):
+        for part in CHUNKS:
             for t in range(4):
-                other_gather(t, k)
-        ctx_gather(3, 0)
-        ctx_gather(3, 1)
-        hid0 = hid_round(0, 0, 384)
-        ctx_gather(3, 2)
-        finish(0, 384, hid0, w3_q)
-        hid1 = hid_round(1, 0, 384)
-        hid2 = hid_round(2, 0, 128)
-        finish(384, 384, hid1, w3_q)
-        hid3 = hid_round(2, 128, 128)
-        finish(768, 128, hid2, w3_q)
-        finish(896, 128, hid3, w3_q)
+                y_gather(t, u2_sb, part)
+        hid = [hid_round(CHUNKS[0])]
+        for k, part in enumerate(CHUNKS):
+            if k + 1 < len(CHUNKS):
+                hid.append(hid_round(CHUNKS[k + 1]))
+            finish(part, hid[k], w3_q)

from contextlib import ExitStack

import concourse.mybir as mybir

F32 = mybir.dt.float32
BF16 = mybir.dt.bfloat16
I32 = mybir.dt.int32
U32 = mybir.dt.uint32
U16 = mybir.dt.uint16
U8 = mybir.dt.uint8
FP8X4 = mybir.dt.float8_e4m3fn_x4
COPY = mybir.ActivationFunctionType.Copy
ADD = mybir.AluOpType.add
MULT = mybir.AluOpType.mult

P = 128
T, S, H, N, U = 2048, 512, 512, 128, 1024
FLOPS = 2 * (2 * 512 * H * S + H * N * U)
PAD = 16
HALVES = [(0, 512), (512, 512)]
CHUNKS = [(0, 384), (384, 384), (768, 128), (896, 128)]


def tile_picked_ybackpt_ctx_p_kernel(
    tc, x_words, x_scales, w1, w2, unit, w3, offs, u1, u2, out
):
    nc = tc.nc
    with ExitStack() as ctx:
        keep = ctx.enter_context(tc.tile_pool(name="keep", bufs=1))
        acc_pool = ctx.enter_context(tc.psum_pool(name="acc", bufs=1))
        out_pool = ctx.enter_context(tc.psum_pool(name="res", bufs=3))

        offs_sb = keep.tile([P, S // 16], U16, name="offs_sb")
        u1_sb = keep.tile([P, U // 16], U16, name="u1_sb")
        u2_sb = keep.tile([P, U // 16], U16, name="u2_sb")
        unit_sb = keep.tile([P, 4], F32, name="unit_sb")
        x_word_table = keep.tile([P, T], I32, name="x_word_table")
        x_scale_table = keep.tile([P, T], U8, name="x_scale_table")
        w1_raw = keep.tile([P, 4, H], F32, name="w1_raw")
        w2_raw = keep.tile([P, 4, H], F32, name="w2_raw")
        w3_raw = keep.tile([P, 4, N], F32, name="w3_raw")

        nc.vector.memset(x_scale_table[:].bitcast(I32), 0)
        nc.scalar.dma_start(out=unit_sb[:], in_=unit.rearrange("(p t) one -> p (t one)", t=4))
        nc.sync.dma_start(out=w1_raw[:], in_=w1.rearrange("(p j) c -> p j c", j=4))
        for r in range(4):
            nc.sync.dma_start(
                out=x_scale_table[r:P:32, :].bitcast(I32),
                in_=x_scales[0].rearrange("(q r) c -> r q c", r=4)[r].bitcast(I32),
            )
        nc.sync.dma_start(offs_sb[:], offs)
        nc.sync.dma_start(out=x_word_table[:], in_=x_words[0].rearrange("p n t -> p (n t)").bitcast(I32))
        nc.sync.dma_start(u1_sb[:], u1)
        nc.sync.dma_start(out=w2_raw[:], in_=w2.rearrange("(p j) c -> p j c", j=4))
        nc.sync.dma_start(u2_sb[:], u2)
        nc.sync.dma_start(out=w3_raw[:], in_=w3.rearrange("(p j) c -> p j c", j=4))

        cross_gain = keep.tile([P, 4], F32, name="cross_gain")
        nc.scalar.activation(cross_gain[:], unit_sb[:], COPY, scale=-0.6)

        def pair_tile(name):
            return keep.tile([P, 2, P, 4], BF16, name=name, align_bytes=64)

        def round_pair(copy, grouped, rows, raw, pair):
            copy(
                out=grouped[:, :, rows, :].rearrange("p e m j -> p m j e"),
                in_=raw[:].rearrange("p j (m u e) -> p u m j e", u=2, e=2)[:, pair],
            )

        def flat(grouped):
            return grouped[:].rearrange("p e m j -> p (e m j)")

        def quantise(grouped, width, name):
            codes = keep.tile([P, width], U32, name=name + "_codes", align_bytes=64)
            scales = keep.tile([P, width], U8, name=name + "_scales", align_bytes=64)
            nc.vector.quantize_mx(out=codes[:].bitcast(FP8X4), scales=scales[:], in_=grouped)
            return codes, scales

        def product(dst, lhs, lhs_cols, rhs, rhs_cols):
            nc.tensor.matmul_mx(
                out=dst,
                lhsT=lhs[0][:, lhs_cols].bitcast(FP8X4),
                lhsT_scale=lhs[1][:, lhs_cols],
                rhs=rhs[0][:, rhs_cols].bitcast(FP8X4),
                rhs_scale=rhs[1][:, rhs_cols],
                start=True,
                stop=True,
            )

        w1_pairs = [pair_tile("w1_lo"), pair_tile("w1_hi")]
        round_pair(nc.vector.tensor_copy, w1_pairs[0], slice(0, P), w1_raw, 0)
        round_pair(nc.scalar.copy, w1_pairs[1], slice(0, P), w1_raw, 1)
        w1_q = [quantise(flat(w1_pairs[0]), 2 * P, "w1_lo"), quantise(flat(w1_pairs[1]), 2 * P, "w1_hi")]

        x_bytes = keep.tile([P, S], U8, name="x_bytes", align_bytes=64)
        nc.vector.tensor_copy(x_bytes[:], x_scale_table[:].indirect(offs_sb[:]))
        x_codes = keep.tile([P, S], U32, name="x_codes", align_bytes=64)
        for h in range(2):
            nc.vector.tensor_copy(
                x_codes[:, h * 256 : (h + 1) * 256],
                x_word_table[:].bitcast(U32).indirect(offs_sb[:, h * 16 : (h + 1) * 16]),
            )
        x_q = (x_codes, x_bytes)

        def project(w_q, t, bank):
            acc = acc_pool.tile([P, S], F32, name="acc%d" % bank)
            product(acc[:], w_q[t // 2], slice((t % 2) * P, (t % 2 + 1) * P), x_q, slice(0, S))
            return acc

        def window(name):
            win = keep.tile([P, S + PAD], F32, name=name, align_bytes=64)
            nc.vector.memset(win[:, S:], 0.0)
            return win

        def picks(list_sb, part):
            first, n = part
            return list_sb[:, first // 16 : (first + n) // 16]

        def cols(tile, t, part):
            first, n = part
            return tile[:, t, first : first + n]

        picked_y = keep.tile([P, 4, U], F32, name="picked_y")
        rep = keep.tile([P, 4, U], F32, name="rep")
        ctxh = keep.tile([P, 4, U], F32, name="ctxh")
        y_win = [window("y_win%d" % t) for t in range(4)]
        z_win = [window("z_win%d" % t) for t in range(4)]
        c_win = [window("c_win%d" % t) for t in range(4)]

        def y_stage(t, y_acc):
            nc.scalar.activation(y_win[t][:, 0:S], y_acc[:], COPY, scale=unit_sb[:, t : t + 1])

        def y_gather(t, list_sb, part):
            nc.scalar.activation(cols(picked_y, t, part), y_win[t][:].indirect(picks(list_sb, part)), COPY)

        def rep_gather(t, part):
            nc.vector.tensor_tensor(
                cols(rep, t, part), c_win[t][:].indirect(picks(u2_sb, part)), cols(picked_y, t, part), ADD
            )

        def ctx_gather(t, part):
            nc.vector.tensor_tensor(
                cols(ctxh, t, part), z_win[t][:].indirect(picks(u1_sb, part)), cols(rep, t, part), MULT
            )

        def hid_round(part):
            first, n = part
            hid = keep.tile([P, n, 4], BF16, name="hid%d" % first, align_bytes=64)
            nc.vector.tensor_tensor(
                hid[:].rearrange("p (c i) t -> p c t i", i=4),
                ctxh[:, :, first : first + n].rearrange("p t (c i) -> p c t i", i=4),
                picked_y[:, :, first : first + n].rearrange("p t (c i) -> p c t i", i=4),
                ADD,
            )
            return hid[:].rearrange("p r t -> p (r t)")

        def finish(part, hid, w3_q):
            first, n = part
            hid_q = quantise(hid, n, "hid%d" % first)
            res = out_pool.tile([P, n], F32, name="res")
            for a in range(0, n, 256):
                piece = slice(a, min(a + 256, n))
                product(res[:, piece], w3_q, slice(0, N), hid_q, piece)
            res_sb = keep.tile([P, n], F32, name="res_sb%d" % first)
            nc.scalar.copy(out=res_sb[:], in_=res[:])
            queue = nc.scalar if first + n == U else nc.sync
            queue.dma_start(out=out[:, first : first + n], in_=res_sb[:])

        for h in range(2):
            half = slice(h * 256, (h + 1) * 256)
            acc = acc_pool.tile([P, 256], F32, name="acc%d" % (3 * h))
            product(acc[:], w1_q[0], slice(0, P), x_q, half)
            nc.scalar.activation(y_win[0][:, half], acc[:], COPY, scale=unit_sb[:, 0:1])
        for part in HALVES:
            y_gather(0, u1_sb, part)

        w2_pair = pair_tile("w2_pair")
        round_pair(nc.vector.tensor_copy, w2_pair, slice(0, P), w2_raw, 0)
        w2_first = quantise(flat(w2_pair)[:, 0 : 4 * P], P, "w2_first")
        w2_second = quantise(flat(w2_pair)[:, 4 * P : 8 * P], P, "w2_second")
        w2_pair = pair_tile("w2_pair")
        round_pair(nc.vector.tensor_copy, w2_pair, slice(0, P), w2_raw, 1)
        z_halves = []
        for h in range(2):
            half = slice(h * 256, (h + 1) * 256)
            acc = acc_pool.tile([P, 256], F32, name="acc%d" % (1 + 3 * h))
            product(acc[:], w2_first, slice(0, P), x_q, half)
            nc.vector.tensor_scalar(c_win[0][:, half], acc[:], cross_gain[:, 0:1], None, MULT)
            z_halves.append(acc)
        for h in range(2):
            nc.scalar.copy(out=z_win[0][:, h * 256 : (h + 1) * 256], in_=z_halves[h][:])
        w2_hi = quantise(flat(w2_pair), 2 * P, "w2_hi")
        w2_q = [None, (w2_second, 0), (w2_hi, 0), (w2_hi, P)]
        z_acc = [None]
        for t in range(1, 4):
            acc = acc_pool.tile([P, S], F32, name="acc%d" % ((t + 1) % 4))
            product(acc[:], w2_q[t][0], slice(w2_q[t][1], w2_q[t][1] + P), x_q, slice(0, S))
            z_acc.append(acc)

        for t in range(4):
            if t > 0:
                nc.scalar.copy(out=z_win[t][:, 0:S], in_=z_acc[t][:])
                y_stage(t, project(w1_q, t, t))
                if t == 1:
                    nc.vector.tensor_scalar(c_win[t][:, 0:S], z_win[t][:, 0:S], cross_gain[:, t : t + 1], None, MULT)
                else:
                    nc.scalar.activation(c_win[t][:, 0:S], z_acc[t][:], COPY, scale=cross_gain[:, t : t + 1])
                for part in HALVES:
                    y_gather(t, u1_sb, part)
            for part in HALVES:
                rep_gather(t, part)
            for part in HALVES:
                ctx_gather(t, part)

        w3_grouped = keep.tile([P, N, 4], BF16, name="w3_grouped", tag="z_win1", align_bytes=64)
        nc.scalar.copy(
            out=w3_grouped[:].rearrange("p (c i) j -> p c j i", i=4),
            in_=w3_raw[:].rearrange("p j (c i) -> p c j i", i=4),
        )
        w3_q = quantise(w3_grouped[:].rearrange("p m j -> p (m j)"), N, "w3")

        for part in CHUNKS:
            for t in range(4):
                y_gather(t, u2_sb, part)
        hid = [hid_round(CHUNKS[0])]
        for k, part in enumerate(CHUNKS):
            if k + 1 < len(CHUNKS):
                hid.append(hid_round(CHUNKS[k + 1]))
            finish(part, hid[k], w3_q)
